import numpy as np
import ml_dtypes


def mxq(x, axis, fmt="e4m3"):
    dtype, down = {"e4m3": (ml_dtypes.float8_e4m3fn, 7), "e5m2": (ml_dtypes.float8_e5m2, 14)}[fmt]
    v = np.moveaxis(np.asarray(x, np.float32).astype(ml_dtypes.bfloat16).astype(np.float64), axis, -1)
    blocks = v.reshape(v.shape[:-1] + (-1, 32))
    amax = np.abs(blocks).max(-1, keepdims=True)
    byte = np.maximum(np.where(amax > 0, np.frexp(amax)[1] - 1 + 127, 0) - down, 1)
    scale = np.exp2(byte - 127.0)
    codes = (blocks / scale).astype(np.float32).astype(dtype).astype(np.float64)
    return np.moveaxis((codes * scale).reshape(v.shape), -1, axis)


WIDE = False


def mx_kscale(k):
    if not WIDE:
        return np.ones(k)
    levels = np.array([10, -10, 5, -5, 0])
    if k % 512:
        return np.exp2(np.random.permutation(np.resize(levels, k // 32))).repeat(32)
    a = np.empty((k // 512, 16))
    for p in range(k // 512):
        a[p, :8] = np.random.permutation(np.resize(levels, 8))
        for g in range(8):
            far = levels[np.abs(levels - a[p, g]) >= 10]
            a[p, g + 8] = far[np.random.randint(len(far))]
    return np.exp2(a.ravel()).repeat(32)


def f64(x):
    return np.asarray(x).astype(np.float64)


def striped8(idx):
    return np.concatenate([x.reshape(-1, 16).T for x in idx]).astype(np.uint16)


def runs(offs, k):
    lists = np.stack([offs[16 * r : 16 * r + 16].T.reshape(-1) for r in range(8)]).astype(np.int64)
    return lists[np.arange(k) % 512 // 64]


def pack_weight(w):
    k, n = w.shape
    w = f64(np.asarray(w, np.float32).astype(ml_dtypes.bfloat16)).reshape(k // 32, 32, n)
    amax = np.abs(w).max(1)
    byte = np.clip(np.where(amax > 0, np.frexp(amax)[1] - 1 + 127 - 7, 1), 1, 254)
    scaled = (w * np.exp2(127.0 - byte)[:, None, :]).reshape(k, n).astype(np.float32)
    words = np.ascontiguousarray(scaled.reshape(k // 512, 128, 4, n).transpose(0, 1, 3, 2)).astype(ml_dtypes.float8_e4m3fn).view(np.uint8)
    return words, np.ascontiguousarray(byte.astype(np.uint8).reshape(k // 512, 16, n))


def unpack_weight(words, scales):
    g, p, n, _ = words.shape
    vals = np.ascontiguousarray(words).view(ml_dtypes.float8_e4m3fn).astype(np.float64) * np.repeat(np.exp2(scales.astype(np.float64) - 127.0), 8, axis=1)[..., None]
    return vals.transpose(0, 1, 3, 2).reshape(g * 512, n)


def sigmoid(v):
    return 1.0 / (1.0 + np.exp(-np.maximum(v, -700.0)))


K, T, S, N = 512, 2048, 512, 512


def setup_inputs():
    n = np.random.standard_normal
    s = mx_kscale(K)[:, None]
    packed_xT = pack_weight(n((K, T)) * s)
    return {
        "x_words": packed_xT[0],
        "x_scales": packed_xT[1],
        "hid": n((N, S)).astype(np.float32),
        "w1": (n((K, N)) / np.sqrt(K) / s).astype(np.float32),
        "w2": (n((K, N)) / np.sqrt(K) / s).astype(np.float32),
        "offs": striped8(np.random.randint(0, T, (8, S))),
    }


def reference(x_words, x_scales, hid, w1, w2, offs):
    xq = unpack_weight(x_words, x_scales)[np.arange(K)[:, None], runs(offs, K)]
    s = sigmoid(f64(hid) * ((mxq(f64(w1), 0, "e4m3").T @ xq)))
    val = mxq(f64(w2), 0, "e4m3").T @ xq
    return f64(hid) + s * val

@@ -1,0 +1,130 @@
+from contextlib import ExitStack
+
+import concourse.mybir as mybir
+
+K, T, S, N = 512, 2048, 512, 512
+FLOPS = 2 * 2 * K * S * N
+
+F32 = mybir.dt.float32
+BF16 = mybir.dt.bfloat16
+I32 = mybir.dt.int32
+U32 = mybir.dt.uint32
+U16 = mybir.dt.uint16
+U8 = mybir.dt.uint8
+FP8X4 = mybir.dt.float8_e4m3fn_x4
+MULT = mybir.AluOpType.mult
+ADD = mybir.AluOpType.add
+SIGMOID = mybir.ActivationFunctionType.Sigmoid
+
+P = 128
+PACK = 4
+HALF = N // 2
+
+
+def tile_picked_engramh_none_p_kernel(tc, x_words, x_scales, hid, w1, w2, offs, out):
+    nc = tc.nc
+    with ExitStack() as ctx:
+        keep = ctx.enter_context(tc.tile_pool(name="keep", bufs=1))
+        psum = ctx.enter_context(tc.psum_pool(name="psum", bufs=1))
+
+        def load_weight(raw, w, half):
+            nc.sync.dma_start(raw.rearrange("p (t m) -> p t m", t=PACK),
+                              w.rearrange("(p t) m -> p t m", t=PACK)[:, :, half * HALF : (half + 1) * HALF])
+            return raw
+
+        def load_hid(rows, block):
+            nc.sync.dma_start(rows, hid[block * P : (block + 1) * P, :])
+            return rows
+
+        def quantise(raw, name, copy):
+            grouped = keep.tile([P, HALF, PACK], BF16, name=f"grouped_{name}", tag=f"grouped_{name}", align_bytes=64)
+            copy(grouped[:].rearrange("p (c i) t -> p c t i", i=4), raw.rearrange("p (t c i) -> p c t i", t=PACK, i=4))
+            codes = keep.tile([P, HALF], U32, name=f"codes_{name}", align_bytes=64)
+            plane = keep.tile([P, HALF], U8, name=f"plane_{name}", align_bytes=64)
+            nc.vector.quantize_mx(out=codes[:].bitcast(FP8X4), scales=plane[:], in_=grouped[:].rearrange("p m t -> p (m t)"))
+            return codes, plane
+
+        def product(weights, sub, name):
+            codes, plane = weights
+            cols = slice(sub * P, (sub + 1) * P)
+            bank = psum.tile([P, S], F32, name=name)
+            nc.tensor.matmul_mx(out=bank[:], lhsT=codes[:, cols].bitcast(FP8X4), lhsT_scale=plane[:, cols],
+                                rhs=x_codes[:].bitcast(FP8X4), rhs_scale=x_plane[:], start=True, stop=True)
+            return bank
+
+        def gate_of(key, rows, block):
+            pre = keep.tile([P, S], F32, name=f"pre{block}")
+            nc.vector.tensor_tensor(pre[:], key[:], rows, MULT)
+            gate = keep.tile([P, S], F32, name=f"gate{block}")
+            nc.scalar.activation(gate[:], pre[:], SIGMOID)
+            return gate
+
+        def finish(val, gate, rows, block, engine):
+            gated = keep.tile([P, S], F32, name=f"gated{block}")
+            nc.vector.tensor_tensor(gated[:], val[:], gate[:], MULT)
+            result = keep.tile([P, S], F32, name=f"result{block}")
+            engine.tensor_tensor(result[:], gated[:], rows, ADD)
+            nc.sync.dma_start(out[block * P : (block + 1) * P, :], result[:])
+
+
+        offsets = keep.tile([P, S // 16], U16, name="offsets")
+        nc.sync.dma_start(offsets[:], offs)
+        early_k = keep.tile([P, PACK * HALF], F32, name="early_k", align_bytes=64)
+        raw_k0 = load_weight(early_k[:], w1, 0)
+
+        scale_table = keep.tile([P, T], U8, name="scale_table", tag="reused", align_bytes=64)
+        nc.vector.memset(scale_table[:].bitcast(I32), 0)
+        scale_rows = x_scales[0].bitcast(I32)
+        for e in range(2):
+            nc.sync.dma_start(scale_table[e:P:16, :].bitcast(I32), scale_rows[e:16:2, :])
+
+        x_plane = keep.tile([P, S], U8, name="x_plane", align_bytes=64)
+        nc.vector.memset(x_plane[:].bitcast(I32), 0)
+        warm = keep.tile([P, 2], F32, name="warm")
+        nc.vector.memset(warm[:, 0:1], 0.0)
+        nc.scalar.activation(warm[:, 1:2], warm[:, 0:1], SIGMOID)
+
+        word_table = keep.tile([P, T], U32, name="word_table", align_bytes=64)
+        nc.sync.dma_start(word_table[:].bitcast(I32), x_words[0].rearrange("p n t -> p (n t)").bitcast(I32))
+        early_v = keep.tile([P, PACK * HALF], F32, name="early_v", align_bytes=64)
+        raw_v0 = load_weight(early_v[:], w2, 0)
+
+        picked_bytes = keep.tile([P, S], U8, name="picked_bytes", align_bytes=64)
+        nc.vector.tensor_copy(picked_bytes[:], scale_table[:].indirect(offsets[:]))
+        for e in range(2):
+            nc.sync.dma_start(x_plane[2 + e : P : 32, :].bitcast(I32), picked_bytes[16 + e : P : 32, :].bitcast(I32))
+        for q in range(4):
+            nc.vector.tensor_copy(x_plane[32 * q : 32 * q + 2, :].bitcast(I32), picked_bytes[32 * q : 32 * q + 2, :].bitcast(I32))
+
+        late = keep.tile([P, 2 * PACK * HALF + 4 * S], F32, name="late", tag="reused", align_bytes=64)
+        hid0 = load_hid(late[:, 0:512], 0)
+        hid1 = load_hid(late[:, 512:1024], 1)
+        raw_k1 = load_weight(late[:, 1024:2048], w1, 1)
+        hid2 = load_hid(late[:, 2048:2560], 2)
+        raw_v1 = load_weight(late[:, 2560:3584], w2, 1)
+        hid3 = load_hid(late[:, 3584:4096], 3)
+
+        wk0 = quantise(raw_k0, "k0", nc.scalar.copy)
+
+        x_codes = keep.tile([P, S], U32, name="x_codes", align_bytes=64)
+        nc.vector.tensor_copy(x_codes[:], word_table[:].indirect(offsets[:]))
+
+        key0 = product(wk0, 0, "key0")
+        key1 = product(wk0, 1, "key1")
+        wv0 = quantise(raw_v0, "v0", nc.scalar.copy)
+        gate0 = gate_of(key0, hid0, 0)
+        val0 = product(wv0, 0, "val0")
+        val1 = product(wv0, 1, "val1")
+        gate1 = gate_of(key1, hid1, 1)
+        wk1 = quantise(raw_k1, "k1", nc.scalar.copy)
+        key2 = product(wk1, 0, "key2")
+        key3 = product(wk1, 1, "key3")
+        finish(val0, gate0, hid0, 0, nc.gpsimd)
+        finish(val1, gate1, hid1, 1, nc.gpsimd)
+        wv1 = quantise(raw_v1, "v1", nc.vector.tensor_copy)
+        gate2 = gate_of(key2, hid2, 2)
+        gate3 = gate_of(key3, hid3, 3)
+        val2 = product(wv1, 0, "val2")
+        val3 = product(wv1, 1, "val3")
+        finish(val2, gate2, hid2, 2, nc.gpsimd)
+        finish(val3, gate3, hid3, 3, nc.vector)

@@ -18,7 +18,7 @@ SIGMOID = mybir.ActivationFunctionType.Sigmoid
 
 P = 128
 PACK = 4
-HALF = N // 2
+BLOCKS = N // P
 
 
 def tile_picked_engramh_none_p_kernel(tc, x_words, x_scales, hid, w1, w2, offs, out):
@@ -27,28 +27,34 @@ def tile_picked_engramh_none_p_kernel(tc, x_words, x_scales, hid, w1, w2, offs, 
         keep = ctx.enter_context(tc.tile_pool(name="keep", bufs=1))
         psum = ctx.enter_context(tc.psum_pool(name="psum", bufs=1))
 
-        def load_weight(raw, w, half):
-            nc.sync.dma_start(raw.rearrange("p (t m) -> p t m", t=PACK),
-                              w.rearrange("(p t) m -> p t m", t=PACK)[:, :, half * HALF : (half + 1) * HALF])
+        def load_weight(raw, w, first, count):
+            raw = raw.rearrange("p (t m) -> p t m", t=PACK)
+            nc.sync.dma_start(raw, w.rearrange("(p t) m -> p t m", t=PACK)[:, :, first * P : (first + count) * P])
             return raw
 
         def load_hid(rows, block):
             nc.sync.dma_start(rows, hid[block * P : (block + 1) * P, :])
             return rows
 
-        def quantise(raw, name, copy):
-            grouped = keep.tile([P, HALF, PACK], BF16, name=f"grouped_{name}", tag=f"grouped_{name}", align_bytes=64)
-            copy(grouped[:].rearrange("p (c i) t -> p c t i", i=4), raw.rearrange("p (t c i) -> p c t i", t=PACK, i=4))
-            codes = keep.tile([P, HALF], U32, name=f"codes_{name}", align_bytes=64)
-            plane = keep.tile([P, HALF], U8, name=f"plane_{name}", align_bytes=64)
-            nc.vector.quantize_mx(out=codes[:].bitcast(FP8X4), scales=plane[:], in_=grouped[:].rearrange("p m t -> p (m t)"))
-            return codes, plane
+        def interleave(raw, grouped, copy):
+            copy(grouped.rearrange("p (c i t) -> p c t i", i=4, t=PACK), raw.rearrange("p t (c i) -> p c t i", i=4))
 
-        def product(weights, sub, name):
+        def quantise(grouped, name):
+            width = grouped.shape[1] // PACK
+            codes = keep.tile([P, width], U32, name=f"codes_{name}", align_bytes=64)
+            plane = keep.tile([P, width], U8, name=f"plane_{name}", align_bytes=64)
+            nc.vector.quantize_mx(out=codes[:].bitcast(FP8X4), scales=plane[:], in_=grouped)
+            return [(codes[:, c : c + P], plane[:, c : c + P]) for c in range(0, width, P)]
+
+        def prepare(raw, name, copy):
+            grouped = keep.tile([P, PACK * raw.shape[2]], BF16, name=f"grouped_{name}", align_bytes=64)
+            interleave(raw, grouped[:], copy)
+            return quantise(grouped[:], name)
+
+        def product(weights, name):
             codes, plane = weights
-            cols = slice(sub * P, (sub + 1) * P)
             bank = psum.tile([P, S], F32, name=name)
-            nc.tensor.matmul_mx(out=bank[:], lhsT=codes[:, cols].bitcast(FP8X4), lhsT_scale=plane[:, cols],
+            nc.tensor.matmul_mx(out=bank[:], lhsT=codes.bitcast(FP8X4), lhsT_scale=plane,
                                 rhs=x_codes[:].bitcast(FP8X4), rhs_scale=x_plane[:], start=True, stop=True)
             return bank
 
@@ -59,24 +65,27 @@ def tile_picked_engramh_none_p_kernel(tc, x_words, x_scales, hid, w1, w2, offs, 
             nc.scalar.activation(gate[:], pre[:], SIGMOID)
             return gate
 
-        def finish(val, gate, rows, block, engine):
+        def apply_gate(val, gate, block):
             gated = keep.tile([P, S], F32, name=f"gated{block}")
             nc.vector.tensor_tensor(gated[:], val[:], gate[:], MULT)
-            result = keep.tile([P, S], F32, name=f"result{block}")
-            engine.tensor_tensor(result[:], gated[:], rows, ADD)
-            nc.sync.dma_start(out[block * P : (block + 1) * P, :], result[:])
+            return gated
 
+        def finish(gated, rows, block, engine, parts):
+            width = S // parts
+            for part in range(parts):
+                cols = slice(part * width, (part + 1) * width)
+                result = keep.tile([P, width], F32, name=f"result{block}_{part}")
+                engine.tensor_tensor(result[:], gated[:, cols], rows[:, cols], ADD)
+                nc.sync.dma_start(out[block * P : (block + 1) * P, cols], result[:])
 
         offsets = keep.tile([P, S // 16], U16, name="offsets")
         nc.sync.dma_start(offsets[:], offs)
-        early_k = keep.tile([P, PACK * HALF], F32, name="early_k", align_bytes=64)
-        raw_k0 = load_weight(early_k[:], w1, 0)
+        early = keep.tile([P, 4 * S], F32, name="early", align_bytes=64)
+        raw_k0 = load_weight(early[:, 0:512], w1, 0, 1)
 
         scale_table = keep.tile([P, T], U8, name="scale_table", tag="reused", align_bytes=64)
         nc.vector.memset(scale_table[:].bitcast(I32), 0)
-        scale_rows = x_scales[0].bitcast(I32)
-        for e in range(2):
-            nc.sync.dma_start(scale_table[e:P:16, :].bitcast(I32), scale_rows[e:16:2, :])
+        nc.sync.dma_start(scale_table[0:P:8, :].bitcast(I32), x_scales[0].bitcast(I32))
 
         x_plane = keep.tile([P, S], U8, name="x_plane", align_bytes=64)
         nc.vector.memset(x_plane[:].bitcast(I32), 0)
@@ -86,45 +95,46 @@ def tile_picked_engramh_none_p_kernel(tc, x_words, x_scales, hid, w1, w2, offs, 
 
         word_table = keep.tile([P, T], U32, name="word_table", align_bytes=64)
         nc.sync.dma_start(word_table[:].bitcast(I32), x_words[0].rearrange("p n t -> p (n t)").bitcast(I32))
-        early_v = keep.tile([P, PACK * HALF], F32, name="early_v", align_bytes=64)
-        raw_v0 = load_weight(early_v[:], w2, 0)
+        raw_k1 = load_weight(early[:, 512:1024], w1, 1, 1)
+        hid0 = load_hid(early[:, 1024:1536], 0)
+        raw_v0 = load_weight(early[:, 1536:2048], w2, 0, 1)
 
         picked_bytes = keep.tile([P, S], U8, name="picked_bytes", align_bytes=64)
         nc.vector.tensor_copy(picked_bytes[:], scale_table[:].indirect(offsets[:]))
-        for e in range(2):
-            nc.sync.dma_start(x_plane[2 + e : P : 32, :].bitcast(I32), picked_bytes[16 + e : P : 32, :].bitcast(I32))
-        for q in range(4):
-            nc.vector.tensor_copy(x_plane[32 * q : 32 * q + 2, :].bitcast(I32), picked_bytes[32 * q : 32 * q + 2, :].bitcast(I32))
+        for i in range(4):
+            nc.sync.dma_start(x_plane[i:P:32, :].bitcast(I32), picked_bytes[8 * i : P : 32, :].bitcast(I32))
 
-        late = keep.tile([P, 2 * PACK * HALF + 4 * S], F32, name="late", tag="reused", align_bytes=64)
-        hid0 = load_hid(late[:, 0:512], 0)
-        hid1 = load_hid(late[:, 512:1024], 1)
-        raw_k1 = load_weight(late[:, 1024:2048], w1, 1)
+        late = keep.tile([P, 8 * S], F32, name="late", tag="reused", align_bytes=64)
+        raw_k23 = load_weight(late[:, 0:1024], w1, 2, 2)
+        hid1 = load_hid(late[:, 1024:1536], 1)
+        raw_v1 = load_weight(late[:, 1536:2048], w2, 1, 1)
         hid2 = load_hid(late[:, 2048:2560], 2)
-        raw_v1 = load_weight(late[:, 2560:3584], w2, 1)
+        raw_v23 = load_weight(late[:, 2560:3584], w2, 2, 2)
         hid3 = load_hid(late[:, 3584:4096], 3)
 
-        wk0 = quantise(raw_k0, "k0", nc.scalar.copy)
+        on_scalar, on_vector = nc.scalar.copy, nc.vector.tensor_copy
+        (wk0,) = prepare(raw_k0, "k0", on_scalar)
 
         x_codes = keep.tile([P, S], U32, name="x_codes", align_bytes=64)
         nc.vector.tensor_copy(x_codes[:], word_table[:].indirect(offsets[:]))
 
-        key0 = product(wk0, 0, "key0")
-        key1 = product(wk0, 1, "key1")
-        wv0 = quantise(raw_v0, "v0", nc.scalar.copy)
+        key0 = product(wk0, "key0")
+        key1 = product(prepare(raw_k1, "k1", on_scalar)[0], "key1")
+        val0 = product(prepare(raw_v0, "v0", on_scalar)[0], "val0")
         gate0 = gate_of(key0, hid0, 0)
-        val0 = product(wv0, 0, "val0")
-        val1 = product(wv0, 1, "val1")
+        key2 = product(prepare(raw_k23[:, :, 0:P], "k2", on_scalar)[0], "key2")
         gate1 = gate_of(key1, hid1, 1)
-        wk1 = quantise(raw_k1, "k1", nc.scalar.copy)
-        key2 = product(wk1, 0, "key2")
-        key3 = product(wk1, 1, "key3")
-        finish(val0, gate0, hid0, 0, nc.gpsimd)
-        finish(val1, gate1, hid1, 1, nc.gpsimd)
-        wv1 = quantise(raw_v1, "v1", nc.vector.tensor_copy)
+        gated0 = apply_gate(val0, gate0, 0)
+        val1 = product(prepare(raw_v1, "v1", on_scalar)[0], "val1")
+        finish(gated0, hid0, 0, nc.vector, 1)
         gate2 = gate_of(key2, hid2, 2)
+        key3 = product(prepare(raw_k23[:, :, P : 2 * P], "k3", on_scalar)[0], "key3")
+        gated1 = apply_gate(val1, gate1, 1)
+        val2 = product(prepare(raw_v23[:, :, 0:P], "v2", on_scalar)[0], "val2")
+        finish(gated1, hid1, 1, nc.vector, 1)
         gate3 = gate_of(key3, hid3, 3)
-        val2 = product(wv1, 0, "val2")
-        val3 = product(wv1, 1, "val3")
-        finish(val2, gate2, hid2, 2, nc.gpsimd)
-        finish(val3, gate3, hid3, 3, nc.vector)
+        val3 = product(prepare(raw_v23[:, :, P : 2 * P], "v3", on_scalar)[0], "val3")
+        gated2 = apply_gate(val2, gate2, 2)
+        finish(gated2, hid2, 2, nc.vector, 1)
+        gated3 = apply_gate(val3, gate3, 3)
+        finish(gated3, hid3, 3, nc.vector, 2)

@@ -51,16 +51,22 @@ def tile_picked_engramh_none_p_kernel(tc, x_words, x_scales, hid, w1, w2, offs, 
             interleave(raw, grouped[:], copy)
             return quantise(grouped[:], name)
 
-        def product(weights, name):
+        def multiply(bank, weights, cols):
             codes, plane = weights
-            bank = psum.tile([P, S], F32, name=name)
-            nc.tensor.matmul_mx(out=bank[:], lhsT=codes.bitcast(FP8X4), lhsT_scale=plane,
-                                rhs=x_codes[:].bitcast(FP8X4), rhs_scale=x_plane[:], start=True, stop=True)
+            nc.tensor.matmul_mx(out=bank, lhsT=codes.bitcast(FP8X4), lhsT_scale=plane,
+                                rhs=x_codes[:, cols].bitcast(FP8X4), rhs_scale=x_plane[:, cols], start=True, stop=True)
+
+        def product(weights, name, cols=slice(0, S), tag=None):
+            bank = psum.tile([P, cols.stop - cols.start], F32, name=name, tag=tag or name)
+            multiply(bank[:], weights, cols)
             return bank
 
-        def gate_of(key, rows, block):
+        def gate_of(keys, rows, block):
             pre = keep.tile([P, S], F32, name=f"pre{block}")
-            nc.vector.tensor_tensor(pre[:], key[:], rows, MULT)
+            width = S // len(keys)
+            for part, key in enumerate(keys):
+                cols = slice(part * width, (part + 1) * width)
+                nc.vector.tensor_tensor(pre[:, cols], key[:], rows[:, cols], MULT)
             gate = keep.tile([P, S], F32, name=f"gate{block}")
             nc.scalar.activation(gate[:], pre[:], SIGMOID)
             return gate
@@ -70,9 +76,9 @@ def tile_picked_engramh_none_p_kernel(tc, x_words, x_scales, hid, w1, w2, offs, 
             nc.vector.tensor_tensor(gated[:], val[:], gate[:], MULT)
             return gated
 
-        def finish(gated, rows, block, engine, parts):
-            width = S // parts
-            for part in range(parts):
+        def finish(gated, rows, block, engines):
+            width = S // len(engines)
+            for part, engine in enumerate(engines):
                 cols = slice(part * width, (part + 1) * width)
                 result = keep.tile([P, width], F32, name=f"result{block}_{part}")
                 engine.tensor_tensor(result[:], gated[:, cols], rows[:, cols], ADD)
@@ -80,8 +86,8 @@ def tile_picked_engramh_none_p_kernel(tc, x_words, x_scales, hid, w1, w2, offs, 
 
         offsets = keep.tile([P, S // 16], U16, name="offsets")
         nc.sync.dma_start(offsets[:], offs)
-        early = keep.tile([P, 4 * S], F32, name="early", align_bytes=64)
-        raw_k0 = load_weight(early[:, 0:512], w1, 0, 1)
+        early = keep.tile([P, 5 * S], F32, name="early", align_bytes=64)
+        raw_k01 = load_weight(early[:, 0:1024], w1, 0, 2)
 
         scale_table = keep.tile([P, T], U8, name="scale_table", tag="reused", align_bytes=64)
         nc.vector.memset(scale_table[:].bitcast(I32), 0)
@@ -93,48 +99,55 @@ def tile_picked_engramh_none_p_kernel(tc, x_words, x_scales, hid, w1, w2, offs, 
         nc.vector.memset(warm[:, 0:1], 0.0)
         nc.scalar.activation(warm[:, 1:2], warm[:, 0:1], SIGMOID)
 
+        raw_k23 = load_weight(early[:, 1024:2048], w1, 2, 2)
         word_table = keep.tile([P, T], U32, name="word_table", align_bytes=64)
         nc.sync.dma_start(word_table[:].bitcast(I32), x_words[0].rearrange("p n t -> p (n t)").bitcast(I32))
-        raw_k1 = load_weight(early[:, 512:1024], w1, 1, 1)
-        hid0 = load_hid(early[:, 1024:1536], 0)
-        raw_v0 = load_weight(early[:, 1536:2048], w2, 0, 1)
+        raw_v0 = load_weight(early[:, 2048:2560], w2, 0, 1)
 
         picked_bytes = keep.tile([P, S], U8, name="picked_bytes", align_bytes=64)
         nc.vector.tensor_copy(picked_bytes[:], scale_table[:].indirect(offsets[:]))
         for i in range(4):
             nc.sync.dma_start(x_plane[i:P:32, :].bitcast(I32), picked_bytes[8 * i : P : 32, :].bitcast(I32))
 
-        late = keep.tile([P, 8 * S], F32, name="late", tag="reused", align_bytes=64)
-        raw_k23 = load_weight(late[:, 0:1024], w1, 2, 2)
+        late = keep.tile([P, 7 * S], F32, name="late", tag="reused", align_bytes=64)
+        hid0 = load_hid(late[:, 0:512], 0)
+        raw_v1 = load_weight(late[:, 512:1024], w2, 1, 1)
         hid1 = load_hid(late[:, 1024:1536], 1)
-        raw_v1 = load_weight(late[:, 1536:2048], w2, 1, 1)
-        hid2 = load_hid(late[:, 2048:2560], 2)
-        raw_v23 = load_weight(late[:, 2560:3584], w2, 2, 2)
-        hid3 = load_hid(late[:, 3584:4096], 3)
+        raw_v2 = load_weight(late[:, 1536:2048], w2, 2, 1)
+        raw_v3 = load_weight(late[:, 2048:2560], w2, 3, 1)
+        hid2 = load_hid(late[:, 2560:3072], 2)
+        hid3 = load_hid(late[:, 3072:3584], 3)
 
         on_scalar, on_vector = nc.scalar.copy, nc.vector.tensor_copy
-        (wk0,) = prepare(raw_k0, "k0", on_scalar)
+        wk = prepare(raw_k01, "k01", on_scalar) + prepare(raw_k23, "k23", on_scalar)
 
         x_codes = keep.tile([P, S], U32, name="x_codes", align_bytes=64)
-        nc.vector.tensor_copy(x_codes[:], word_table[:].indirect(offsets[:]))
+        halves = (slice(0, S // 2), slice(S // 2, S))
+        for cols in halves:
+            nc.vector.tensor_copy(x_codes[:, cols], word_table[:].indirect(offsets[:, cols.start // 16 : cols.stop // 16]))
 
-        key0 = product(wk0, "key0")
-        key1 = product(prepare(raw_k1, "k1", on_scalar)[0], "key1")
+        key1 = psum.tile([P, S], F32, name="key1")
+        key0a = product(wk[0], "key0a", halves[0])
+        multiply(key1[:, halves[0]], wk[1], halves[0])
+        key0 = [key0a, product(wk[0], "key0b", halves[1])]
+        multiply(key1[:, halves[1]], wk[1], halves[1])
         val0 = product(prepare(raw_v0, "v0", on_scalar)[0], "val0")
+        key2 = product(wk[2], "key2")
         gate0 = gate_of(key0, hid0, 0)
-        key2 = product(prepare(raw_k23[:, :, 0:P], "k2", on_scalar)[0], "key2")
-        gate1 = gate_of(key1, hid1, 1)
-        gated0 = apply_gate(val0, gate0, 0)
         val1 = product(prepare(raw_v1, "v1", on_scalar)[0], "val1")
-        finish(gated0, hid0, 0, nc.vector, 1)
-        gate2 = gate_of(key2, hid2, 2)
-        key3 = product(prepare(raw_k23[:, :, P : 2 * P], "k3", on_scalar)[0], "key3")
-        gated1 = apply_gate(val1, gate1, 1)
-        val2 = product(prepare(raw_v23[:, :, 0:P], "v2", on_scalar)[0], "val2")
-        finish(gated1, hid1, 1, nc.vector, 1)
-        gate3 = gate_of(key3, hid3, 3)
-        val3 = product(prepare(raw_v23[:, :, P : 2 * P], "v3", on_scalar)[0], "val3")
+        gate1 = gate_of([key1], hid1, 1)
+        finish(apply_gate(val0, gate0, 0), hid0, 0, [nc.gpsimd])
+        grouped_v23 = keep.tile([P, 2 * S], BF16, name="grouped_v23", align_bytes=64)
+        interleave(raw_v2, grouped_v23[:, 0:S], on_scalar)
+        interleave(raw_v3, grouped_v23[:, S : 2 * S], on_scalar)
+        gate2 = gate_of([key2], hid2, 2)
+        finish(apply_gate(val1, gate1, 1), hid1, 1, [nc.gpsimd])
+        key3 = product(wk[3], "key3", tag="key2")
+        gate3 = gate_of([key3], hid3, 3)
+        wv23 = quantise(grouped_v23[:], "v23")
+        val2 = product(wv23[0], "val2")
+        val3 = product(wv23[1], "val3")
         gated2 = apply_gate(val2, gate2, 2)
-        finish(gated2, hid2, 2, nc.vector, 1)
         gated3 = apply_gate(val3, gate3, 3)
-        finish(gated3, hid3, 3, nc.vector, 2)
+        finish(gated2, hid2, 2, [nc.gpsimd, nc.vector])
+        finish(gated3, hid3, 3, [nc.vector, nc.vector])

from contextlib import ExitStack

import concourse.mybir as mybir

K, T, S, N = 512, 2048, 512, 512
FLOPS = 2 * 2 * K * S * N

F32 = mybir.dt.float32
BF16 = mybir.dt.bfloat16
I32 = mybir.dt.int32
U32 = mybir.dt.uint32
U16 = mybir.dt.uint16
U8 = mybir.dt.uint8
FP8X4 = mybir.dt.float8_e4m3fn_x4
MULT = mybir.AluOpType.mult
ADD = mybir.AluOpType.add
SIGMOID = mybir.ActivationFunctionType.Sigmoid

P = 128
PACK = 4
BLOCKS = N // P


def tile_picked_engramh_none_p_kernel(tc, x_words, x_scales, hid, w1, w2, offs, out):
    nc = tc.nc
    with ExitStack() as ctx:
        keep = ctx.enter_context(tc.tile_pool(name="keep", bufs=1))
        psum = ctx.enter_context(tc.psum_pool(name="psum", bufs=1))

        def load_weight(raw, w, first, count):
            raw = raw.rearrange("p (t m) -> p t m", t=PACK)
            nc.sync.dma_start(raw, w.rearrange("(p t) m -> p t m", t=PACK)[:, :, first * P : (first + count) * P])
            return raw

        def load_hid(rows, block):
            nc.sync.dma_start(rows, hid[block * P : (block + 1) * P, :])
            return rows

        def interleave(raw, grouped, copy):
            copy(grouped.rearrange("p (c i t) -> p c t i", i=4, t=PACK), raw.rearrange("p t (c i) -> p c t i", i=4))

        def quantise(grouped, name):
            width = grouped.shape[1] // PACK
            codes = keep.tile([P, width], U32, name=f"codes_{name}", align_bytes=64)
            plane = keep.tile([P, width], U8, name=f"plane_{name}", align_bytes=64)
            nc.vector.quantize_mx(out=codes[:].bitcast(FP8X4), scales=plane[:], in_=grouped)
            return [(codes[:, c : c + P], plane[:, c : c + P]) for c in range(0, width, P)]

        def prepare(raw, name, copy):
            grouped = keep.tile([P, PACK * raw.shape[2]], BF16, name=f"grouped_{name}", align_bytes=64)
            interleave(raw, grouped[:], copy)
            return quantise(grouped[:], name)

        def multiply(bank, weights, cols):
            codes, plane = weights
            nc.tensor.matmul_mx(out=bank, lhsT=codes.bitcast(FP8X4), lhsT_scale=plane,
                                rhs=x_codes[:, cols].bitcast(FP8X4), rhs_scale=x_plane[:, cols], start=True, stop=True)

        def product(weights, name, cols=slice(0, S), tag=None):
            bank = psum.tile([P, cols.stop - cols.start], F32, name=name, tag=tag or name)
            multiply(bank[:], weights, cols)
            return bank

        def gate_of(keys, rows, block):
            pre = keep.tile([P, S], F32, name=f"pre{block}")
            width = S // len(keys)
            for part, key in enumerate(keys):
                cols = slice(part * width, (part + 1) * width)
                nc.vector.tensor_tensor(pre[:, cols], key[:], rows[:, cols], MULT)
            gate = keep.tile([P, S], F32, name=f"gate{block}")
            nc.scalar.activation(gate[:], pre[:], SIGMOID)
            return gate

        def apply_gate(val, gate, block):
            gated = keep.tile([P, S], F32, name=f"gated{block}")
            nc.vector.tensor_tensor(gated[:], val[:], gate[:], MULT)
            return gated

        def finish(gated, rows, block, engines):
            width = S // len(engines)
            for part, engine in enumerate(engines):
                cols = slice(part * width, (part + 1) * width)
                result = keep.tile([P, width], F32, name=f"result{block}_{part}")
                engine.tensor_tensor(result[:], gated[:, cols], rows[:, cols], ADD)
                nc.sync.dma_start(out[block * P : (block + 1) * P, cols], result[:])

        offsets = keep.tile([P, S // 16], U16, name="offsets")
        nc.sync.dma_start(offsets[:], offs)
        early = keep.tile([P, 5 * S], F32, name="early", align_bytes=64)
        raw_k01 = load_weight(early[:, 0:1024], w1, 0, 2)

        scale_table = keep.tile([P, T], U8, name="scale_table", tag="reused", align_bytes=64)
        nc.vector.memset(scale_table[:].bitcast(I32), 0)
        nc.sync.dma_start(scale_table[0:P:8, :].bitcast(I32), x_scales[0].bitcast(I32))

        x_plane = keep.tile([P, S], U8, name="x_plane", align_bytes=64)
        nc.vector.memset(x_plane[:].bitcast(I32), 0)
        warm = keep.tile([P, 2], F32, name="warm")
        nc.vector.memset(warm[:, 0:1], 0.0)
        nc.scalar.activation(warm[:, 1:2], warm[:, 0:1], SIGMOID)

        raw_k23 = load_weight(early[:, 1024:2048], w1, 2, 2)
        word_table = keep.tile([P, T], U32, name="word_table", align_bytes=64)
        nc.sync.dma_start(word_table[:].bitcast(I32), x_words[0].rearrange("p n t -> p (n t)").bitcast(I32))
        raw_v0 = load_weight(early[:, 2048:2560], w2, 0, 1)

        picked_bytes = keep.tile([P, S], U8, name="picked_bytes", align_bytes=64)
        nc.vector.tensor_copy(picked_bytes[:], scale_table[:].indirect(offsets[:]))
        for i in range(4):
            nc.sync.dma_start(x_plane[i:P:32, :].bitcast(I32), picked_bytes[8 * i : P : 32, :].bitcast(I32))

        late = keep.tile([P, 7 * S], F32, name="late", tag="reused", align_bytes=64)
        hid0 = load_hid(late[:, 0:512], 0)
        raw_v1 = load_weight(late[:, 512:1024], w2, 1, 1)
        hid1 = load_hid(late[:, 1024:1536], 1)
        raw_v2 = load_weight(late[:, 1536:2048], w2, 2, 1)
        raw_v3 = load_weight(late[:, 2048:2560], w2, 3, 1)
        hid2 = load_hid(late[:, 2560:3072], 2)
        hid3 = load_hid(late[:, 3072:3584], 3)

        on_scalar, on_vector = nc.scalar.copy, nc.vector.tensor_copy
        wk = prepare(raw_k01, "k01", on_scalar) + prepare(raw_k23, "k23", on_scalar)

        x_codes = keep.tile([P, S], U32, name="x_codes", align_bytes=64)
        halves = (slice(0, S // 2), slice(S // 2, S))
        for cols in halves:
            nc.vector.tensor_copy(x_codes[:, cols], word_table[:].indirect(offsets[:, cols.start // 16 : cols.stop // 16]))

        key1 = psum.tile([P, S], F32, name="key1")
        key0a = product(wk[0], "key0a", halves[0])
        multiply(key1[:, halves[0]], wk[1], halves[0])
        key0 = [key0a, product(wk[0], "key0b", halves[1])]
        multiply(key1[:, halves[1]], wk[1], halves[1])
        val0 = product(prepare(raw_v0, "v0", on_scalar)[0], "val0")
        key2 = product(wk[2], "key2")
        gate0 = gate_of(key0, hid0, 0)
        val1 = product(prepare(raw_v1, "v1", on_scalar)[0], "val1")
        gate1 = gate_of([key1], hid1, 1)
        finish(apply_gate(val0, gate0, 0), hid0, 0, [nc.gpsimd])
        grouped_v23 = keep.tile([P, 2 * S], BF16, name="grouped_v23", align_bytes=64)
        interleave(raw_v2, grouped_v23[:, 0:S], on_scalar)
        interleave(raw_v3, grouped_v23[:, S : 2 * S], on_scalar)
        gate2 = gate_of([key2], hid2, 2)
        finish(apply_gate(val1, gate1, 1), hid1, 1, [nc.gpsimd])
        key3 = product(wk[3], "key3", tag="key2")
        gate3 = gate_of([key3], hid3, 3)
        wv23 = quantise(grouped_v23[:], "v23")
        val2 = product(wv23[0], "val2")
        val3 = product(wv23[1], "val3")
        gated2 = apply_gate(val2, gate2, 2)
        gated3 = apply_gate(val3, gate3, 3)
        finish(gated2, hid2, 2, [nc.gpsimd, nc.vector])
        finish(gated3, hid3, 3, [nc.vector, nc.vector])
